import numpy as np
CORES = [0,4,8,12,16,20,24,28,32,36,40,44,48,52,56,60,64,68,72,76,80,84,88,92,96,100,104,108,112,116,120,124,128,132,136,140,144,148,152,156,160,164,168,172,176,180,184,188,192,196,200,204,208,212,216,220,224,228,232,236,240,244,248,252,256,260,264,268,272,276,280,284,288,292,296,300,304,308,312,316,320,324,328,332,336,340,344,348,352,356,360,364,368,372,376,380,384,388,392,396,400,404,408,412,416,420,424,428,432,436,440,444,448,452,456,460,464,468,472,476,480,484,488,492,496,500,504,508]
N = 128
TOK, D = 8, 256
ROUTE = [[[77,92],[45,126],[98,107],[64,77],[53,54],[64,82],[17,77],[24,77]],[[8,52],[56,110],[41,77],[4,126],[15,77],[77,109],[61,77],[20,74]],[[7,49],[5,77],[98,122],[44,77],[100,108],[15,113],[32,77],[36,106]],[[21,33],[77,122],[2,77],[77,117],[62,77],[68,77],[3,83],[77,111]],[[21,116],[57,77],[71,77],[1,24],[90,94],[68,108],[79,104],[28,96]],[[77,81],[78,92],[66,117],[77,96],[10,48],[56,84],[12,77],[9,31]],[[96,105],[37,93],[77,126],[60,102],[22,69],[55,77],[77,103],[77,116]],[[77,93],[33,123],[42,114],[21,39],[71,123],[4,56],[47,75],[22,113]],[[80,98],[67,94],[16,102],[1,77],[33,45],[20,78],[59,67],[15,88]],[[77,115],[120,127],[2,121],[69,113],[36,83],[78,88],[7,91],[5,37]],[[27,77],[20,92],[45,89],[40,77],[53,82],[46,118],[58,82],[71,101]],[[78,83],[56,77],[107,115],[77,82],[32,77],[70,119],[59,77],[41,77]],[[70,77],[77,79],[26,77],[47,92],[62,122],[52,116],[15,54],[25,28]],[[46,77],[0,77],[51,77],[76,77],[3,61],[8,57],[23,77],[20,44]],[[40,81],[2,32],[49,77],[56,77],[5,13],[42,90],[35,82],[6,25]],[[0,53],[67,91],[17,36],[15,52],[96,118],[13,114],[77,88],[76,77]],[[27,92],[44,74],[68,77],[83,115],[7,80],[77,83],[118,124],[9,23]],[[77,85],[17,118],[42,64],[70,82],[77,94],[77,126],[9,77],[77,86]],[[18,77],[34,77],[5,25],[33,89],[37,115],[68,106],[13,98],[71,77]],[[52,77],[73,109],[75,77],[17,25],[77,90],[77,98],[37,117],[77,105]],[[64,77],[30,126],[77,89],[70,77],[59,126],[22,60],[7,77],[112,125]],[[0,59],[14,77],[4,56],[65,77],[5,77],[35,116],[62,77],[77,111]],[[35,89],[77,127],[31,117],[70,116],[25,77],[77,86],[4,79],[41,77]],[[37,77],[97,111],[60,77],[46,95],[69,77],[7,107],[77,86],[6,123]],[[77,80],[67,77],[22,77],[77,127],[73,77],[77,120],[39,115],[78,115]],[[68,77],[31,77],[9,104],[11,77],[82,91],[77,100],[56,104],[77,99]],[[69,115],[98,118],[60,77],[69,77],[62,99],[77,96],[14,77],[39,127]],[[1,65],[77,109],[50,77],[7,14],[99,126],[70,78],[77,78],[19,77]],[[83,90],[77,114],[33,56],[29,124],[1,77],[77,117],[0,77],[1,11]],[[76,125],[13,36],[50,116],[31,69],[77,126],[87,127],[54,97],[97,106]],[[104,110],[61,66],[77,98],[22,118],[54,77],[72,99],[11,47],[51,125]],[[77,85],[59,77],[18,127],[8,93],[28,77],[77,113],[65,72],[17,77]],[[69,77],[77,111],[59,84],[43,57],[77,126],[77,89],[20,77],[12,77]],[[10,49],[45,49],[60,115],[14,56],[24,109],[97,114],[77,86],[77,84]],[[13,77],[42,46],[12,121],[36,48],[77,98],[77,104],[38,77],[40,86]],[[43,77],[62,77],[47,77],[77,88],[21,77],[38,119],[69,114],[77,113]],[[27,29],[29,101],[62,118],[48,77],[77,78],[48,88],[34,77],[64,97]],[[30,81],[39,56],[82,106],[31,98],[28,39],[23,77],[64,123],[46,77]],[[77,95],[15,77],[77,126],[73,101],[37,104],[9,77],[53,80],[77,120]],[[34,81],[15,74],[11,124],[77,120],[2,92],[5,123],[10,22],[74,77]],[[119,121],[77,106],[29,117],[58,72],[4,26],[73,85],[10,63],[56,77]],[[26,67],[72,107],[75,77],[58,118],[30,77],[0,77],[45,68],[77,112]],[[48,93],[3,55],[25,77],[46,61],[1,77],[77,90],[108,118],[22,77]],[[63,86],[9,77],[40,77],[93,94],[20,77],[18,60],[77,100],[77,123]],[[14,95],[77,106],[77,90],[35,77],[37,77],[5,77],[20,77],[77,87]],[[13,77],[77,124],[52,121],[77,123],[77,79],[5,77],[83,118],[32,37]],[[38,77],[77,95],[33,77],[77,80],[20,70],[72,77],[77,80],[7,124]],[[77,119],[17,77],[73,77],[60,77],[90,101],[29,77],[77,96],[28,77]],[[59,96],[77,115],[77,91],[96,102],[12,77],[100,122],[42,77],[9,107]],[[76,106],[61,96],[89,123],[40,77],[105,107],[37,39],[0,77],[65,77]],[[18,106],[51,77],[2,77],[8,41],[77,117],[79,119],[5,61],[45,77]],[[77,81],[77,92],[77,82],[105,122],[77,97],[32,126],[74,104],[114,115]],[[44,122],[56,61],[41,75],[4,82],[77,97],[49,104],[77,105],[41,77]],[[52,77],[2,83],[77,112],[25,77],[6,26],[63,77],[77,82],[12,69]],[[77,126],[77,79],[54,83],[7,77],[57,76],[61,77],[77,84],[45,77]],[[33,109],[72,102],[49,69],[28,56],[77,78],[23,110],[26,42],[77,97]],[[5,68],[2,41],[46,92],[59,77],[77,100],[0,77],[68,98],[20,61]],[[44,77],[46,77],[77,85],[3,48],[77,84],[53,77],[45,109],[0,2]],[[79,105],[77,95],[20,77],[77,124],[3,123],[32,43],[77,112],[97,122]],[[6,18],[58,66],[77,78],[30,125],[62,77],[31,106],[77,89],[37,77]],[[33,77],[77,118],[77,105],[69,77],[77,89],[21,108],[77,85],[13,27]],[[40,72],[50,118],[120,127],[77,110],[10,89],[74,77],[62,77],[61,77]],[[33,77],[20,77],[77,78],[10,77],[26,77],[8,23],[77,97],[100,103]],[[51,63],[11,77],[81,107],[11,101],[57,77],[28,77],[31,43],[34,77]],[[77,122],[14,15],[10,103],[57,123],[77,79],[77,101],[86,114],[2,40]],[[71,85],[64,77],[28,98],[72,113],[10,100],[44,101],[77,127],[7,18]],[[25,74],[4,111],[35,44],[65,84],[77,100],[77,83],[77,126],[39,77]],[[17,81],[21,78],[43,99],[69,77],[19,77],[30,101],[36,65],[15,77]],[[62,92],[17,55],[49,77],[30,77],[20,71],[1,77],[57,77],[59,123]],[[62,77],[42,77],[77,99],[17,123],[26,81],[69,126],[55,70],[46,70]],[[77,98],[39,123],[51,77],[77,101],[18,77],[77,111],[44,77],[37,56]],[[77,99],[77,93],[32,77],[20,78],[98,113],[53,75],[69,102],[30,77]],[[50,89],[2,77],[3,79],[77,80],[77,111],[12,45],[62,115],[52,77]],[[77,104],[60,77],[74,110],[20,83],[71,77],[18,76],[19,23],[56,77]],[[77,114],[3,44],[16,77],[8,100],[2,77],[75,77],[77,112],[93,125]],[[15,52],[77,119],[3,73],[59,104],[12,77],[68,79],[6,21],[77,121]],[[2,77],[30,77],[34,77],[38,77],[3,112],[7,81],[62,72],[14,39]],[[47,53],[39,122],[14,82],[62,93],[37,40],[29,77],[70,77],[24,80]],[[19,77],[64,77],[56,90],[49,77],[27,50],[45,77],[34,122],[70,77]],[[19,121],[40,77],[58,77],[77,108],[76,127],[14,77],[85,122],[77,82]],[[65,107],[77,117],[38,58],[17,108],[77,91],[36,77],[53,77],[14,111]],[[76,77],[46,77],[24,48],[66,102],[7,101],[65,77],[75,77],[26,37]],[[59,95],[45,66],[24,77],[63,89],[47,77],[69,126],[41,77],[34,77]],[[69,77],[33,75],[14,40],[77,94],[14,41],[36,65],[1,104],[77,91]],[[77,94],[77,81],[5,36],[77,78],[58,82],[2,68],[3,12],[100,125]],[[41,77],[55,77],[42,77],[52,84],[27,103],[77,81],[77,103],[23,104]],[[77,96],[13,88],[88,112],[11,51],[1,126],[1,77],[77,119],[15,77]],[[9,96],[77,113],[35,115],[63,104],[60,100],[54,77],[77,93],[29,50]],[[59,115],[12,106],[44,77],[47,62],[86,87],[80,109],[4,33],[5,77]],[[22,89],[76,114],[73,77],[60,73],[35,74],[77,120],[54,77],[55,77]],[[26,77],[6,77],[6,12],[34,91],[6,118],[36,77],[82,103],[83,120]],[[58,77],[89,116],[37,86],[77,122],[77,119],[77,125],[23,77],[77,102]],[[54,77],[1,47],[12,33],[51,77],[59,87],[50,100],[18,34],[90,94]],[[0,77],[11,77],[32,104],[24,74],[77,90],[52,77],[4,68],[27,77]],[[20,77],[6,11],[77,126],[71,109],[38,77],[77,122],[32,95],[74,77]],[[77,78],[43,77],[1,77],[44,77],[93,96],[37,77],[36,97],[60,67]],[[30,87],[7,77],[48,60],[56,77],[25,52],[77,125],[2,124],[35,77]],[[12,111],[62,77],[77,102],[77,102],[77,100],[77,83],[77,98],[41,77]],[[17,77],[68,77],[47,100],[77,90],[73,88],[77,80],[19,74],[77,103]],[[77,96],[7,62],[34,55],[77,85],[77,114],[77,89],[20,77],[37,77]],[[77,96],[59,115],[65,77],[77,87],[77,122],[23,125],[39,77],[2,77]],[[77,117],[43,77],[22,116],[17,35],[4,77],[77,84],[71,110],[72,77]],[[93,113],[77,115],[77,124],[62,119],[30,77],[32,119],[54,116],[67,97]],[[3,77],[13,77],[5,77],[32,120],[77,85],[21,93],[8,114],[110,115]],[[6,58],[44,77],[42,77],[83,98],[41,62],[39,111],[29,92],[28,77]],[[59,108],[41,105],[77,98],[77,105],[77,105],[11,39],[25,77],[45,77]],[[13,77],[49,77],[2,101],[66,94],[74,77],[57,77],[47,84],[64,77]],[[30,79],[52,77],[103,117],[77,96],[2,77],[69,77],[53,70],[77,118]],[[77,126],[77,101],[65,125],[28,77],[38,59],[52,77],[24,77],[44,77]],[[36,93],[74,77],[32,56],[64,105],[77,104],[25,77],[35,77],[77,81]],[[30,77],[35,76],[24,77],[39,47],[22,105],[47,77],[77,118],[63,101]],[[58,77],[77,97],[8,108],[77,84],[70,127],[77,114],[5,77],[77,83]],[[50,77],[61,84],[7,71],[22,53],[5,77],[34,77],[14,77],[96,107]],[[64,91],[62,74],[36,123],[77,105],[9,77],[39,85],[12,77],[77,116]],[[77,108],[73,99],[3,80],[98,112],[50,92],[15,124],[77,114],[77,102]],[[60,77],[13,77],[44,77],[47,77],[77,81],[64,73],[12,77],[9,94]],[[93,118],[59,77],[77,96],[85,109],[88,97],[34,84],[77,82],[49,77]],[[7,77],[77,101],[12,77],[60,77],[75,102],[48,76],[40,104],[77,81]],[[1,67],[19,66],[70,119],[80,88],[17,121],[77,84],[4,77],[32,77]],[[77,93],[72,110],[100,103],[74,113],[88,104],[34,36],[3,121],[2,82]],[[16,121],[108,111],[77,88],[83,97],[77,81],[77,119],[77,79],[44,84]],[[43,52],[57,77],[19,77],[40,77],[61,77],[11,32],[3,10],[72,91]],[[8,16],[8,61],[33,95],[41,96],[33,56],[21,73],[70,83],[55,65]],[[50,77],[57,116],[24,112],[35,118],[17,77],[25,49],[29,77],[22,41]],[[33,64],[77,108],[17,77],[57,127],[78,100],[3,77],[77,80],[11,77]],[[77,119],[37,82],[70,77],[77,87],[41,77],[77,89],[92,105],[31,77]],[[69,124],[32,77],[53,77],[48,124],[97,107],[45,67],[77,88],[26,122]],[[81,122],[3,109],[51,77],[14,122],[3,33],[77,93],[26,58],[18,77]]]
CAP = 508
def setup_inputs(rng):
    return {"x": rng.standard_normal((N, TOK, D), dtype=np.float32)}
def reference(x):
    y = np.full((N, CAP, D), np.nan, x.dtype)
    fill = [0] * N
    for r in range(N):
        for t in range(TOK):
            for e in ROUTE[r][t]:
                if fill[e] < CAP:
                    y[e][fill[e]] = x[r][t]
                    fill[e] += 1
    return {"y": y}

@@ -1,0 +1,208 @@
+import comms_topo as ct
+
+SCRATCH = {
+    "xs": ("dram", [8, 128, 2], "float32"),
+    "land": ("dram", [508, 128, 2], "float32"),
+}
+SEMAPHORES = ["loaded", "sent", "arrived", "stored"]
+CACHE = {}
+
+
+def make_plan(ROUTE, CORES, cap=8, hot_cap=8):
+    n = len(CORES)
+    host, chip = ct.host, ct.chip
+    par = lambda c: chip(c) % 2
+    core_at = lambda h, c, k: h * 128 + c * 8 + k
+    fill = [0] * n
+    row = {}
+    for r in range(n):
+        for t, es in enumerate(ROUTE[r]):
+            for e in es:
+                row[(r, t, e)] = fill[e]
+                fill[e] += 1
+    hot = CORES[max(range(n), key=lambda e: fill[e])]
+    tokens = [(r, t) for r in range(n) for t in range(len(ROUTE[r]))]
+    via = {}
+    pair = {}
+    total = {0: 0, 1: 0}
+    kinds = {}
+    for (r, t) in tokens:
+        s = CORES[r]
+        hs = host(s)
+        hl = [host(CORES[e]) for e in ROUTE[r][t]]
+        hd = set(hl)
+        X, Rm, Cb = hs ^ 2, hs ^ 1, 3 - hs
+        if X in hd or Cb in hd:
+            total[hs // 2] += 1
+        if Cb in hd or hl.count(X) == 2:
+            pair[(hs, Cb)] = pair.get((hs, Cb), 0) + 1
+            if X in hd:
+                via[(r, t)] = Cb
+        elif X in hd:
+            kinds[(r, t)] = "nat" if Rm in hd else "free"
+    for kind in ("nat", "free"):
+        for (r, t) in tokens:
+            if kinds.get((r, t)) != kind:
+                continue
+            hs = host(CORES[r])
+            X, Rm, Cb = hs ^ 2, hs ^ 1, 3 - hs
+            target = (total[hs // 2] + 1) // 2
+            a, b = ((Rm, X), (hs, Cb)) if kind == "nat" else ((hs, Cb), (Rm, X))
+            p = a if pair.get(a, 0) < target else b
+            pair[p] = pair.get(p, 0) + 1
+            via[(r, t)] = p[0] if p[0] != hs else p[1]
+    load = {}
+    slots = {}
+    first = {c: [] for c in CORES}
+    second = {}
+    arrive = {}
+    selfs = {c: [] for c in CORES}
+
+    def pick(groups, limit=None):
+        for cands in groups:
+            best = None
+            for c in cands:
+                l = load.get(c, 0)
+                if l < (limit or cap) and (best is None or l < load.get(best, 0)):
+                    best = c
+            if best is not None:
+                return best
+        raise ValueError("no relay")
+
+    def helpers(h, c, k0, owner):
+        ks = [k0 + 2, k0 + 3] + ([] if owner else [k0 + 1])
+        k1 = k0 ^ 4
+        ks2 = [k1 + 2, k1 + 3] + ([] if owner else [k1 + 1])
+        return [[core_at(h, c, k) for k in ks], [core_at(h, c, k) for k in ks2]]
+
+    jobs = []
+    for (r, t) in tokens:
+        s = CORES[r]
+        hs, cs, k0 = host(s), chip(s), s % 8
+        ds = []
+        for e in ROUTE[r][t]:
+            d = CORES[e]
+            if d == s:
+                selfs[s].append((t, row[(r, t, e)]))
+            else:
+                ds.append((d, row[(r, t, e)]))
+        br = {}
+        for d, sl in ds:
+            hd = host(d)
+            h1 = via[(r, t)] if hd == hs ^ 2 else hd
+            br.setdefault(h1, []).append((d, sl))
+        direct = []
+        own = []
+        relays = []
+        for h1, B in br.items():
+            inh1 = all(host(d) == h1 for d, _ in B)
+            if inh1 and (len(B) == 1 or h1 == hs):
+                if len(B) == 2 and chip(B[0][0]) == chip(B[1][0]) and chip(B[0][0]) != cs and par(B[0][0]) == par(s):
+                    relays.append((h1, B))
+                    continue
+                for d, sl in B:
+                    if par(d) == par(s):
+                        direct.append((d, sl))
+                    else:
+                        own.append((d, sl))
+            else:
+                relays.append((h1, B))
+        jobs.append((r, t, s, direct, own, relays))
+
+    rls = [[] for _ in jobs]
+    hm = [core_at(host(hot), chip(hot) ^ 1, k) for k in (2, 3, 6, 7)]
+    hotchipmate = (host(hot), chip(hot) ^ 1)
+
+    def own_pass(sel):
+        for j, (r, t, s, direct, own, relays) in enumerate(jobs):
+            if own and sel(s):
+                rc = pick(helpers(host(s), chip(s), s % 8, True), hot_cap if (host(s), chip(s)) == hotchipmate else None)
+                load[rc] = load.get(rc, 0) + 1
+                rls[j].append((rc, list(own)))
+                del own[:]
+
+    own_pass(lambda s: (host(s), chip(s)) == hotchipmate)
+    for j, (r, t, s, direct, own, relays) in enumerate(jobs):
+        for x in list(own):
+            if x[0] == hot and host(s) // 2 == host(hot) // 2:
+                k0 = s % 8
+                c2 = [c for c in hm if c % 8 // 4 == k0 // 4]
+                try:
+                    rc = pick([c2], hot_cap)
+                except ValueError:
+                    continue
+                own.remove(x)
+                load[rc] = load.get(rc, 0) + 1
+                rls[j].append((rc, [x]))
+    own_pass(lambda s: True)
+    for j, (r, t, s, direct, own, relays) in enumerate(jobs):
+        hs, cs, k0 = host(s), chip(s), s % 8
+        dsts = list(direct)
+        rl = rls[j]
+        for h1, B in relays:
+            owner = any(par(d) != par(s) for d, _ in B)
+            groups = []
+            for d, _ in B:
+                if host(d) == h1 and par(d) == par(s):
+                    groups += helpers(h1, chip(d), d % 8, owner)
+            groups += helpers(h1, cs, k0, owner)
+            for dc in range(2, 16, 2):
+                groups += helpers(h1, (cs + dc) % 16, k0, owner)
+            rc = pick(groups)
+            load[rc] = load.get(rc, 0) + 1
+            rl.append((rc, B))
+        for rc, B in rl:
+            sl = slots.get(rc, 0)
+            slots[rc] = sl + 1
+            dsts.append((rc, sl))
+            second.setdefault(rc, []).append((sl, B))
+        first[s].append((t, dsts))
+    for prog in (first, second):
+        for c, trs in prog.items():
+            for _, dsts in trs:
+                for d, _ in dsts:
+                    arrive[d] = arrive.get(d, 0) + 1
+    return dict(first=first, second=second, arrive=arrive, selfs=selfs, fill=fill, pair=pair)
+
+
+def send(g, core, T, topo, src, transfers):
+    from concourse.bass import DstId, RemoteDMATransfer
+    for i in range(0, len(transfers), 8):
+        trs = []
+        for j, (sl, dsts) in enumerate(transfers[i:i + 8]):
+            ids = []
+            for d, _ in dsts:
+                rid, pid = topo.addr(d, core)
+                ids.append(DstId(rid=rid, pnc=pid))
+            trs.append(RemoteDMATransfer(dst_ids=ids, dma_engine_mask=1 << j, remote_sem=T.sem.arrived,
+                                         srcs=[src[sl]], dsts=[T.land[x] for _, x in dsts]))
+        g.remote_dma_fused(trs, local_sem=T.sem.sent)
+    return len(transfers)
+
+
+def rank_program(g, core, T, topo):
+    if "plan" not in CACHE:
+        CACHE["plan"] = make_plan(T.tables["ROUTE"], list(T.cores))
+    P = CACHE["plan"]
+    rank = T.rank_of(core)
+    arrive = P["arrive"].get(core, 0)
+    if rank is None:
+        trs = P["second"].get(core)
+        if not trs:
+            return
+        g.wait_ge(T.sem.arrived, arrive)
+        k = send(g, core, T, topo, T.land, trs)
+        g.wait_ge(T.sem.sent, k)
+        return
+    g.dma_start(T.xs[:], T.x[:]).then_inc(T.sem.loaded, 16)
+    nl = 16
+    for t, rw in P["selfs"][core]:
+        g.dma_start(T.land[rw], T.x[t]).then_inc(T.sem.loaded, 16)
+        nl += 16
+    g.wait_ge(T.sem.loaded, nl)
+    k = send(g, core, T, topo, T.xs, P["first"][core])
+    g.wait_ge(T.sem.arrived, arrive)
+    cnt = P["fill"][rank]
+    g.dma_start(T.y[0:cnt], T.land[0:cnt]).then_inc(T.sem.stored, 16)
+    g.wait_ge(T.sem.sent, k)
+    g.wait_ge(T.sem.stored, 16)

@@ -1,208 +1,280 @@
 import comms_topo as ct
 
+TOK, CAP = 8, 508
 SCRATCH = {
-    "xs": ("dram", [8, 128, 2], "float32"),
-    "land": ("dram", [508, 128, 2], "float32"),
+    "xs": ("dram", [TOK, 128, 2], "float32"),
+    "land": ("dram", [CAP, 128, 2], "float32"),
 }
 SEMAPHORES = ["loaded", "sent", "arrived", "stored"]
 CACHE = {}
 
+host, chip, die = ct.host, ct.chip, ct.die
 
-def make_plan(ROUTE, CORES, cap=8, hot_cap=8):
+
+def cid(c):
+    return c // 8
+
+
+def rack(c):
+    return ct.rack(host(c))
+
+
+def par(c):
+    return chip(c) % 2
+
+
+def choose_hosts(ROUTE, CORES, tokens, busiest):
+    via, load, total, shared, free = {}, {}, {0: 0, 1: 0}, [], []
+    for r, t in tokens:
+        hs = host(CORES[r])
+        hl = [host(CORES[e]) for e in ROUTE[r][t]]
+        diag, mate, cabled = hs ^ 2, hs ^ 1, 3 - hs
+        if diag in hl or cabled in hl:
+            total[hs // 2] += 1
+        if cabled in hl or hl.count(diag) == 2:
+            load[(hs, cabled)] = load.get((hs, cabled), 0) + 1
+            if diag in hl:
+                via[(r, t)] = cabled
+        elif diag in hl:
+            (shared if mate in hl else free).append((r, t))
+    bound = (max(total.values()) + 1) // 2
+    two = [sum(1 for es in ROUTE[r] if r not in es and sorted(host(CORES[e]) ^ host(CORES[r]) for e in es) == [0, 2])
+           for r in range(len(CORES))]
+    for hs in range(4):
+        mine = [x for x in shared if host(CORES[x[0]]) == hs]
+        a, b = (hs ^ 1, hs ^ 2), (hs, 3 - hs)
+        while mine and load.get(a, 0) + len(mine) > bound:
+            x = min(mine, key=lambda x: (busiest in ROUTE[x[0]][x[1]], two[x[0]], x))
+            mine.remove(x)
+            two[x[0]] += 1
+            via[x] = b[1]
+            load[b] = load.get(b, 0) + 1
+        for x in mine:
+            via[x] = a[0]
+            load[a] = load.get(a, 0) + 1
+    for x in free:
+        hs = host(CORES[x[0]])
+        a, b = (hs, 3 - hs), (hs ^ 1, hs ^ 2)
+        if load.get(a, 0) < bound:
+            via[x] = a[1]
+            load[a] = load.get(a, 0) + 1
+        else:
+            via[x] = b[0]
+            load[b] = load.get(b, 0) + 1
+    return via, load, bound
+
+
+def make_plan(ROUTE, CORES, writes, chip_cap, seed):
     n = len(CORES)
-    host, chip = ct.host, ct.chip
-    par = lambda c: chip(c) % 2
-    core_at = lambda h, c, k: h * 128 + c * 8 + k
+    tokens = [(r, t) for r in range(n) for t in range(len(ROUTE[r]))]
     fill = [0] * n
     row = {}
+    for r, t in tokens:
+        for e in ROUTE[r][t]:
+            row[(r, t, e)] = fill[e]
+            fill[e] += 1
+    busiest = max(range(n), key=lambda e: fill[e])
+    hot = CORES[busiest]
+    via, load, bound = choose_hosts(ROUTE, CORES, tokens, busiest)
+
+    local = {c: [] for c in CORES}
+    back = set()
     for r in range(n):
-        for t, es in enumerate(ROUTE[r]):
-            for e in es:
-                row[(r, t, e)] = fill[e]
-                fill[e] += 1
-    hot = CORES[max(range(n), key=lambda e: fill[e])]
-    tokens = [(r, t) for r in range(n) for t in range(len(ROUTE[r]))]
-    via = {}
-    pair = {}
-    total = {0: 0, 1: 0}
-    kinds = {}
-    for (r, t) in tokens:
+        runs = []
+        for t in [t for t in range(len(ROUTE[r])) if r in ROUTE[r][t]]:
+            if runs and runs[-1][-1] == t - 1:
+                runs[-1].append(t)
+            else:
+                runs.append([t])
+        if runs:
+            best = max(runs, key=len)
+            local[CORES[r]] = [(best[0], row[(r, best[0], r)], len(best))]
+            back.update((r, t) for run in runs if run is not best for t in run)
+
+    work = []
+    for r in range(n):
         s = CORES[r]
         hs = host(s)
-        hl = [host(CORES[e]) for e in ROUTE[r][t]]
-        hd = set(hl)
-        X, Rm, Cb = hs ^ 2, hs ^ 1, 3 - hs
-        if X in hd or Cb in hd:
-            total[hs // 2] += 1
-        if Cb in hd or hl.count(X) == 2:
-            pair[(hs, Cb)] = pair.get((hs, Cb), 0) + 1
-            if X in hd:
-                via[(r, t)] = Cb
-        elif X in hd:
-            kinds[(r, t)] = "nat" if Rm in hd else "free"
-    for kind in ("nat", "free"):
-        for (r, t) in tokens:
-            if kinds.get((r, t)) != kind:
-                continue
-            hs = host(CORES[r])
-            X, Rm, Cb = hs ^ 2, hs ^ 1, 3 - hs
-            target = (total[hs // 2] + 1) // 2
-            a, b = ((Rm, X), (hs, Cb)) if kind == "nat" else ((hs, Cb), (Rm, X))
-            p = a if pair.get(a, 0) < target else b
-            pair[p] = pair.get(p, 0) + 1
-            via[(r, t)] = p[0] if p[0] != hs else p[1]
-    load = {}
-    slots = {}
-    first = {c: [] for c in CORES}
-    second = {}
+        own = ("chip", cid(s))
+        mine = []
+        for t in range(len(ROUTE[r])):
+            D = [(CORES[e], row[(r, t, e)]) for e in ROUTE[r][t] if e != r or (r, t) in back]
+            v = via.get((r, t))
+            far = [x for x in D if v is not None and host(x[0]) in (hs ^ 2, v)]
+            near = [x for x in D if x not in far]
+            straight = [x for x in near if x[0] != s and par(x[0]) == par(s)]
+            bent = [x for x in near if x not in straight]
+            br = [(("host", v), far)] if far else []
+            other = None
+            if len(straight) == 2 and cid(near[0][0]) == cid(near[1][0]) != cid(s):
+                br.append((("chip", cid(near[0][0])), near))
+            elif len(near) == 2 and host(near[0][0]) == host(near[1][0]) != hs:
+                br.append((("host", host(near[0][0])), near))
+            else:
+                br += [(None, [x]) for x in straight]
+                if bent:
+                    br.append((own, bent))
+                if len(near) == 2:
+                    other = (0 if bent else 1, [(own, near)])
+                elif far and near and all(host(x[0]) == hs ^ 2 for x in far):
+                    other = (2, [(("host", hs ^ 1), far + near)])
+            mine.append([t, br, other])
+        need = sum(len(x[1]) for x in mine)
+        for x in sorted([x for x in mine if x[2]], key=lambda x: x[2][0]):
+            if need <= writes:
+                break
+            if x[2][0] == 2 and via[(r, x[0])] != hs ^ 1:
+                a, b = (hs, 3 - hs), (hs ^ 1, hs ^ 2)
+                if load.get(b, 0) >= bound:
+                    continue
+                load[a] -= 1
+                load[b] = load.get(b, 0) + 1
+            need -= len(x[1]) - 1
+            x[1] = x[2][1]
+        if need > writes:
+            raise ValueError("a source needs %d writes" % need)
+        work += [(r, t, s, b) for t, br, _ in mine for b in br]
+
+    state, sends, port, second = {}, {}, {0: 0, 1: 0}, {}
+    first = {c: {} for c in CORES}
+
+    def st(c):
+        return state.setdefault(c, dict(tokens=0, writes=0, rack_in=False, rack_out=False))
+
+    def hot_port(a, b):
+        if cid(b) == cid(hot) and rack(a) == rack(b) and cid(a) not in (cid(hot), cid(hot) ^ 1):
+            return die(a)
+        return None
+
+    def count(a, b):
+        if cid(a) != cid(b):
+            sends[cid(a)] = sends.get(cid(a), 0) + 1
+        if hot_port(a, b) is not None:
+            port[hot_port(a, b)] += 1
+
+    def fits(s, H, F):
+        q = st(H)
+        if not ct.may_write(s, H) or q["tokens"] >= 8 or q["writes"] + len(F) > writes:
+            return False
+        if any(d == H or not ct.may_write(H, d) for d, _ in F):
+            return False
+        if (q["rack_in"] or rack(s) != rack(H)) and (q["rack_out"] or any(rack(d) != rack(H) for d, _ in F)):
+            return False
+        return sends.get(cid(H), 0) + sum(cid(d) != cid(H) for d, _ in F) <= chip_cap
+
+    def helpers(c, s, F):
+        out = any(rack(d) != rack(c * 8) for d, _ in F)
+        inn = rack(s) != rack(c * 8)
+
+        def key(H):
+            q = st(H)
+            if q["tokens"]:
+                odd = (out and not q["rack_out"]) + (inn and not q["rack_in"])
+            else:
+                odd = int((H % 8 in (1, 2, 6)) != out) if out or inn else 0
+            busy = max([port[hot_port(H, d)] for d, _ in F if hot_port(H, d) is not None] + [0])
+            return (busy, odd, q["writes"], (H * 7919 + seed * 104729) % 1009, H)
+        owners = sorted([c * 8 + k for k in (2, 3, 6, 7)], key=key)
+        if any(par(d) != c % 2 for d, _ in F):
+            return owners
+        return sorted([c * 8 + k for k in (1, 5)], key=key) + owners
+
+    def candidates(where, s, F):
+        if where[0] == "chip":
+            return helpers(where[1], s, F)
+        base = where[1] * 16
+        chips = []
+        for c in [cid(d) for d, _ in F if host(d) == where[1] and par(d) == par(s)] + [base + chip(s)]:
+            if c not in chips:
+                chips.append(c)
+        rest = [c for c in range(base + par(s), base + 16, 2) if c not in chips]
+        chips += sorted(rest, key=lambda c: (sends.get(c, 0), c))
+        return [H for c in chips if c != cid(hot) or any(cid(d) == c for d, _ in F) for H in helpers(c, s, F)]
+
+    level = lambda w: 0 if w[3][0] is None else 1 if w[3][0][0] == "chip" else 2
+    work.sort(key=lambda w: (level(w), (w[0] * 8 + w[1]) * (1 + 2 * seed) % 1024))
+    for w in work:
+        if level(w) == 2:
+            sends[cid(w[2])] = sends.get(cid(w[2]), 0) + 1
+    for r, t, s, (where, F) in work:
+        dsts = first[s].setdefault(t, [])
+        if where is None:
+            dsts += F
+            count(s, F[0][0])
+            continue
+        for H in candidates(where, s, F):
+            if fits(s, H, F):
+                break
+        else:
+            raise ValueError("no helper for token %d of rank %d" % (t, r))
+        q = st(H)
+        dsts.append((H, q["tokens"]))
+        second.setdefault(H, []).append((q["tokens"], list(F)))
+        q["tokens"] += 1
+        q["writes"] += len(F)
+        q["rack_in"] = q["rack_in"] or rack(s) != rack(H)
+        q["rack_out"] = q["rack_out"] or any(rack(d) != rack(H) for d, _ in F)
+        for d, _ in F:
+            count(H, d)
+    first = {c: sorted(first[c].items()) for c in CORES}
     arrive = {}
-    selfs = {c: [] for c in CORES}
-
-    def pick(groups, limit=None):
-        for cands in groups:
-            best = None
-            for c in cands:
-                l = load.get(c, 0)
-                if l < (limit or cap) and (best is None or l < load.get(best, 0)):
-                    best = c
-            if best is not None:
-                return best
-        raise ValueError("no relay")
-
-    def helpers(h, c, k0, owner):
-        ks = [k0 + 2, k0 + 3] + ([] if owner else [k0 + 1])
-        k1 = k0 ^ 4
-        ks2 = [k1 + 2, k1 + 3] + ([] if owner else [k1 + 1])
-        return [[core_at(h, c, k) for k in ks], [core_at(h, c, k) for k in ks2]]
-
-    jobs = []
-    for (r, t) in tokens:
-        s = CORES[r]
-        hs, cs, k0 = host(s), chip(s), s % 8
-        ds = []
-        for e in ROUTE[r][t]:
-            d = CORES[e]
-            if d == s:
-                selfs[s].append((t, row[(r, t, e)]))
-            else:
-                ds.append((d, row[(r, t, e)]))
-        br = {}
-        for d, sl in ds:
-            hd = host(d)
-            h1 = via[(r, t)] if hd == hs ^ 2 else hd
-            br.setdefault(h1, []).append((d, sl))
-        direct = []
-        own = []
-        relays = []
-        for h1, B in br.items():
-            inh1 = all(host(d) == h1 for d, _ in B)
-            if inh1 and (len(B) == 1 or h1 == hs):
-                if len(B) == 2 and chip(B[0][0]) == chip(B[1][0]) and chip(B[0][0]) != cs and par(B[0][0]) == par(s):
-                    relays.append((h1, B))
-                    continue
-                for d, sl in B:
-                    if par(d) == par(s):
-                        direct.append((d, sl))
-                    else:
-                        own.append((d, sl))
-            else:
-                relays.append((h1, B))
-        jobs.append((r, t, s, direct, own, relays))
-
-    rls = [[] for _ in jobs]
-    hm = [core_at(host(hot), chip(hot) ^ 1, k) for k in (2, 3, 6, 7)]
-    hotchipmate = (host(hot), chip(hot) ^ 1)
-
-    def own_pass(sel):
-        for j, (r, t, s, direct, own, relays) in enumerate(jobs):
-            if own and sel(s):
-                rc = pick(helpers(host(s), chip(s), s % 8, True), hot_cap if (host(s), chip(s)) == hotchipmate else None)
-                load[rc] = load.get(rc, 0) + 1
-                rls[j].append((rc, list(own)))
-                del own[:]
-
-    own_pass(lambda s: (host(s), chip(s)) == hotchipmate)
-    for j, (r, t, s, direct, own, relays) in enumerate(jobs):
-        for x in list(own):
-            if x[0] == hot and host(s) // 2 == host(hot) // 2:
-                k0 = s % 8
-                c2 = [c for c in hm if c % 8 // 4 == k0 // 4]
-                try:
-                    rc = pick([c2], hot_cap)
-                except ValueError:
-                    continue
-                own.remove(x)
-                load[rc] = load.get(rc, 0) + 1
-                rls[j].append((rc, [x]))
-    own_pass(lambda s: True)
-    for j, (r, t, s, direct, own, relays) in enumerate(jobs):
-        hs, cs, k0 = host(s), chip(s), s % 8
-        dsts = list(direct)
-        rl = rls[j]
-        for h1, B in relays:
-            owner = any(par(d) != par(s) for d, _ in B)
-            groups = []
-            for d, _ in B:
-                if host(d) == h1 and par(d) == par(s):
-                    groups += helpers(h1, chip(d), d % 8, owner)
-            groups += helpers(h1, cs, k0, owner)
-            for dc in range(2, 16, 2):
-                groups += helpers(h1, (cs + dc) % 16, k0, owner)
-            rc = pick(groups)
-            load[rc] = load.get(rc, 0) + 1
-            rl.append((rc, B))
-        for rc, B in rl:
-            sl = slots.get(rc, 0)
-            slots[rc] = sl + 1
-            dsts.append((rc, sl))
-            second.setdefault(rc, []).append((sl, B))
-        first[s].append((t, dsts))
     for prog in (first, second):
-        for c, trs in prog.items():
+        for trs in prog.values():
             for _, dsts in trs:
                 for d, _ in dsts:
                     arrive[d] = arrive.get(d, 0) + 1
-    return dict(first=first, second=second, arrive=arrive, selfs=selfs, fill=fill, pair=pair)
+    return dict(first=first, second=second, arrive=arrive, local=local, fill=fill)
+
+
+def best_plan(ROUTE, CORES):
+    for writes in range(TOK, 2 * TOK + 1):
+        for chip_cap in range(40, 129, 2):
+            for seed in range(3):
+                try:
+                    return make_plan(ROUTE, CORES, writes, chip_cap, seed)
+                except ValueError as err:
+                    if "source" in str(err):
+                        break
+            else:
+                continue
+            break
+    raise ValueError("no plan")
 
 
 def send(g, core, T, topo, src, transfers):
     from concourse.bass import DstId, RemoteDMATransfer
-    for i in range(0, len(transfers), 8):
-        trs = []
-        for j, (sl, dsts) in enumerate(transfers[i:i + 8]):
-            ids = []
-            for d, _ in dsts:
-                rid, pid = topo.addr(d, core)
-                ids.append(DstId(rid=rid, pnc=pid))
-            trs.append(RemoteDMATransfer(dst_ids=ids, dma_engine_mask=1 << j, remote_sem=T.sem.arrived,
-                                         srcs=[src[sl]], dsts=[T.land[x] for _, x in dsts]))
-        g.remote_dma_fused(trs, local_sem=T.sem.sent)
-    return len(transfers)
+    trs = []
+    for j, (slot, dsts) in enumerate(transfers):
+        ids = []
+        for d, _ in dsts:
+            rid, pid = topo.addr(d, core)
+            ids.append(DstId(rid=rid, pnc=pid))
+        trs.append(RemoteDMATransfer(dst_ids=ids, dma_engine_mask=1 << j, remote_sem=T.sem.arrived,
+                                     srcs=[src[slot]], dsts=[T.land[x] for _, x in dsts]))
+    g.remote_dma_fused(trs, local_sem=T.sem.sent)
+    return len(trs)
 
 
 def rank_program(g, core, T, topo):
     if "plan" not in CACHE:
-        CACHE["plan"] = make_plan(T.tables["ROUTE"], list(T.cores))
+        CACHE["plan"] = best_plan(T.tables["ROUTE"], list(T.cores))
     P = CACHE["plan"]
     rank = T.rank_of(core)
-    arrive = P["arrive"].get(core, 0)
+    due = P["arrive"].get(core, 0)
     if rank is None:
-        trs = P["second"].get(core)
-        if not trs:
-            return
-        g.wait_ge(T.sem.arrived, arrive)
-        k = send(g, core, T, topo, T.land, trs)
-        g.wait_ge(T.sem.sent, k)
+        if core in P["second"]:
+            g.wait_ge(T.sem.arrived, due)
+            g.wait_ge(T.sem.sent, send(g, core, T, topo, T.land, P["second"][core]))
         return
     g.dma_start(T.xs[:], T.x[:]).then_inc(T.sem.loaded, 16)
-    nl = 16
-    for t, rw in P["selfs"][core]:
-        g.dma_start(T.land[rw], T.x[t]).then_inc(T.sem.loaded, 16)
-        nl += 16
-    g.wait_ge(T.sem.loaded, nl)
-    k = send(g, core, T, topo, T.xs, P["first"][core])
-    g.wait_ge(T.sem.arrived, arrive)
-    cnt = P["fill"][rank]
-    g.dma_start(T.y[0:cnt], T.land[0:cnt]).then_inc(T.sem.stored, 16)
-    g.wait_ge(T.sem.sent, k)
+    loads = 16
+    for t, rw, k in P["local"][core]:
+        g.dma_start(T.land[rw:rw + k], T.x[t:t + k]).then_inc(T.sem.loaded, 16)
+        loads += 16
+    g.wait_ge(T.sem.loaded, loads)
+    left = send(g, core, T, topo, T.xs, P["first"][core])
+    g.wait_ge(T.sem.arrived, due)
+    count = P["fill"][rank]
+    g.dma_start(T.y[0:count], T.land[0:count]).then_inc(T.sem.stored, 16)
+    g.wait_ge(T.sem.sent, left)
     g.wait_ge(T.sem.stored, 16)

@@ -146,8 +146,8 @@ def make_plan(ROUTE, CORES, writes, chip_cap, seed):
             return die(a)
         return None
 
-    def count(a, b):
-        if cid(a) != cid(b):
+    def count(a, b, leaves=True):
+        if leaves and cid(a) != cid(b):
             sends[cid(a)] = sends.get(cid(a), 0) + 1
         if hot_port(a, b) is not None:
             port[hot_port(a, b)] += 1
@@ -208,6 +208,7 @@ def make_plan(ROUTE, CORES, writes, chip_cap, seed):
         else:
             raise ValueError("no helper for token %d of rank %d" % (t, r))
         q = st(H)
+        count(s, H, where[0] == "chip")
         dsts.append((H, q["tokens"]))
         second.setdefault(H, []).append((q["tokens"], list(F)))
         q["tokens"] += 1
@@ -223,21 +224,26 @@ def make_plan(ROUTE, CORES, writes, chip_cap, seed):
             for _, dsts in trs:
                 for d, _ in dsts:
                     arrive[d] = arrive.get(d, 0) + 1
-    return dict(first=first, second=second, arrive=arrive, local=local, fill=fill)
+    return dict(first=first, second=second, arrive=arrive, local=local, fill=fill,
+                cost=max(port.values()) + max(sends.values()))
 
 
 def best_plan(ROUTE, CORES):
     for writes in range(TOK, 2 * TOK + 1):
+        found, met = [], 0
         for chip_cap in range(40, 129, 2):
             for seed in range(3):
                 try:
-                    return make_plan(ROUTE, CORES, writes, chip_cap, seed)
+                    found.append(make_plan(ROUTE, CORES, writes, chip_cap, seed))
                 except ValueError as err:
                     if "source" in str(err):
+                        met = 3
                         break
-            else:
-                continue
-            break
+            met += bool(found)
+            if met >= 3:
+                break
+        if found:
+            return min(found, key=lambda P: P["cost"])
     raise ValueError("no plan")
 
 

import comms_topo as ct

TOK, CAP = 8, 508
SCRATCH = {
    "xs": ("dram", [TOK, 128, 2], "float32"),
    "land": ("dram", [CAP, 128, 2], "float32"),
}
SEMAPHORES = ["loaded", "sent", "arrived", "stored"]
CACHE = {}

host, chip, die = ct.host, ct.chip, ct.die


def cid(c):
    return c // 8


def rack(c):
    return ct.rack(host(c))


def par(c):
    return chip(c) % 2


def choose_hosts(ROUTE, CORES, tokens, busiest):
    via, load, total, shared, free = {}, {}, {0: 0, 1: 0}, [], []
    for r, t in tokens:
        hs = host(CORES[r])
        hl = [host(CORES[e]) for e in ROUTE[r][t]]
        diag, mate, cabled = hs ^ 2, hs ^ 1, 3 - hs
        if diag in hl or cabled in hl:
            total[hs // 2] += 1
        if cabled in hl or hl.count(diag) == 2:
            load[(hs, cabled)] = load.get((hs, cabled), 0) + 1
            if diag in hl:
                via[(r, t)] = cabled
        elif diag in hl:
            (shared if mate in hl else free).append((r, t))
    bound = (max(total.values()) + 1) // 2
    two = [sum(1 for es in ROUTE[r] if r not in es and sorted(host(CORES[e]) ^ host(CORES[r]) for e in es) == [0, 2])
           for r in range(len(CORES))]
    for hs in range(4):
        mine = [x for x in shared if host(CORES[x[0]]) == hs]
        a, b = (hs ^ 1, hs ^ 2), (hs, 3 - hs)
        while mine and load.get(a, 0) + len(mine) > bound:
            x = min(mine, key=lambda x: (busiest in ROUTE[x[0]][x[1]], two[x[0]], x))
            mine.remove(x)
            two[x[0]] += 1
            via[x] = b[1]
            load[b] = load.get(b, 0) + 1
        for x in mine:
            via[x] = a[0]
            load[a] = load.get(a, 0) + 1
    for x in free:
        hs = host(CORES[x[0]])
        a, b = (hs, 3 - hs), (hs ^ 1, hs ^ 2)
        if load.get(a, 0) < bound:
            via[x] = a[1]
            load[a] = load.get(a, 0) + 1
        else:
            via[x] = b[0]
            load[b] = load.get(b, 0) + 1
    return via, load, bound


def make_plan(ROUTE, CORES, writes, chip_cap, seed):
    n = len(CORES)
    tokens = [(r, t) for r in range(n) for t in range(len(ROUTE[r]))]
    fill = [0] * n
    row = {}
    for r, t in tokens:
        for e in ROUTE[r][t]:
            row[(r, t, e)] = fill[e]
            fill[e] += 1
    busiest = max(range(n), key=lambda e: fill[e])
    hot = CORES[busiest]
    via, load, bound = choose_hosts(ROUTE, CORES, tokens, busiest)

    local = {c: [] for c in CORES}
    back = set()
    for r in range(n):
        runs = []
        for t in [t for t in range(len(ROUTE[r])) if r in ROUTE[r][t]]:
            if runs and runs[-1][-1] == t - 1:
                runs[-1].append(t)
            else:
                runs.append([t])
        if runs:
            best = max(runs, key=len)
            local[CORES[r]] = [(best[0], row[(r, best[0], r)], len(best))]
            back.update((r, t) for run in runs if run is not best for t in run)

    work = []
    for r in range(n):
        s = CORES[r]
        hs = host(s)
        own = ("chip", cid(s))
        mine = []
        for t in range(len(ROUTE[r])):
            D = [(CORES[e], row[(r, t, e)]) for e in ROUTE[r][t] if e != r or (r, t) in back]
            v = via.get((r, t))
            far = [x for x in D if v is not None and host(x[0]) in (hs ^ 2, v)]
            near = [x for x in D if x not in far]
            straight = [x for x in near if x[0] != s and par(x[0]) == par(s)]
            bent = [x for x in near if x not in straight]
            br = [(("host", v), far)] if far else []
            other = None
            if len(straight) == 2 and cid(near[0][0]) == cid(near[1][0]) != cid(s):
                br.append((("chip", cid(near[0][0])), near))
            elif len(near) == 2 and host(near[0][0]) == host(near[1][0]) != hs:
                br.append((("host", host(near[0][0])), near))
            else:
                br += [(None, [x]) for x in straight]
                if bent:
                    br.append((own, bent))
                if len(near) == 2:
                    other = (0 if bent else 1, [(own, near)])
                elif far and near and all(host(x[0]) == hs ^ 2 for x in far):
                    other = (2, [(("host", hs ^ 1), far + near)])
            mine.append([t, br, other])
        need = sum(len(x[1]) for x in mine)
        for x in sorted([x for x in mine if x[2]], key=lambda x: x[2][0]):
            if need <= writes:
                break
            if x[2][0] == 2 and via[(r, x[0])] != hs ^ 1:
                a, b = (hs, 3 - hs), (hs ^ 1, hs ^ 2)
                if load.get(b, 0) >= bound:
                    continue
                load[a] -= 1
                load[b] = load.get(b, 0) + 1
            need -= len(x[1]) - 1
            x[1] = x[2][1]
        if need > writes:
            raise ValueError("a source needs %d writes" % need)
        work += [(r, t, s, b) for t, br, _ in mine for b in br]

    state, sends, port, second = {}, {}, {0: 0, 1: 0}, {}
    first = {c: {} for c in CORES}

    def st(c):
        return state.setdefault(c, dict(tokens=0, writes=0, rack_in=False, rack_out=False))

    def hot_port(a, b):
        if cid(b) == cid(hot) and rack(a) == rack(b) and cid(a) not in (cid(hot), cid(hot) ^ 1):
            return die(a)
        return None

    def count(a, b, leaves=True):
        if leaves and cid(a) != cid(b):
            sends[cid(a)] = sends.get(cid(a), 0) + 1
        if hot_port(a, b) is not None:
            port[hot_port(a, b)] += 1

    def fits(s, H, F):
        q = st(H)
        if not ct.may_write(s, H) or q["tokens"] >= 8 or q["writes"] + len(F) > writes:
            return False
        if any(d == H or not ct.may_write(H, d) for d, _ in F):
            return False
        if (q["rack_in"] or rack(s) != rack(H)) and (q["rack_out"] or any(rack(d) != rack(H) for d, _ in F)):
            return False
        return sends.get(cid(H), 0) + sum(cid(d) != cid(H) for d, _ in F) <= chip_cap

    def helpers(c, s, F):
        out = any(rack(d) != rack(c * 8) for d, _ in F)
        inn = rack(s) != rack(c * 8)

        def key(H):
            q = st(H)
            if q["tokens"]:
                odd = (out and not q["rack_out"]) + (inn and not q["rack_in"])
            else:
                odd = int((H % 8 in (1, 2, 6)) != out) if out or inn else 0
            busy = max([port[hot_port(H, d)] for d, _ in F if hot_port(H, d) is not None] + [0])
            return (busy, odd, q["writes"], (H * 7919 + seed * 104729) % 1009, H)
        owners = sorted([c * 8 + k for k in (2, 3, 6, 7)], key=key)
        if any(par(d) != c % 2 for d, _ in F):
            return owners
        return sorted([c * 8 + k for k in (1, 5)], key=key) + owners

    def candidates(where, s, F):
        if where[0] == "chip":
            return helpers(where[1], s, F)
        base = where[1] * 16
        chips = []
        for c in [cid(d) for d, _ in F if host(d) == where[1] and par(d) == par(s)] + [base + chip(s)]:
            if c not in chips:
                chips.append(c)
        rest = [c for c in range(base + par(s), base + 16, 2) if c not in chips]
        chips += sorted(rest, key=lambda c: (sends.get(c, 0), c))
        return [H for c in chips if c != cid(hot) or any(cid(d) == c for d, _ in F) for H in helpers(c, s, F)]

    level = lambda w: 0 if w[3][0] is None else 1 if w[3][0][0] == "chip" else 2
    work.sort(key=lambda w: (level(w), (w[0] * 8 + w[1]) * (1 + 2 * seed) % 1024))
    for w in work:
        if level(w) == 2:
            sends[cid(w[2])] = sends.get(cid(w[2]), 0) + 1
    for r, t, s, (where, F) in work:
        dsts = first[s].setdefault(t, [])
        if where is None:
            dsts += F
            count(s, F[0][0])
            continue
        for H in candidates(where, s, F):
            if fits(s, H, F):
                break
        else:
            raise ValueError("no helper for token %d of rank %d" % (t, r))
        q = st(H)
        count(s, H, where[0] == "chip")
        dsts.append((H, q["tokens"]))
        second.setdefault(H, []).append((q["tokens"], list(F)))
        q["tokens"] += 1
        q["writes"] += len(F)
        q["rack_in"] = q["rack_in"] or rack(s) != rack(H)
        q["rack_out"] = q["rack_out"] or any(rack(d) != rack(H) for d, _ in F)
        for d, _ in F:
            count(H, d)
    first = {c: sorted(first[c].items()) for c in CORES}
    arrive = {}
    for prog in (first, second):
        for trs in prog.values():
            for _, dsts in trs:
                for d, _ in dsts:
                    arrive[d] = arrive.get(d, 0) + 1
    return dict(first=first, second=second, arrive=arrive, local=local, fill=fill,
                cost=max(port.values()) + max(sends.values()))


def best_plan(ROUTE, CORES):
    for writes in range(TOK, 2 * TOK + 1):
        found, met = [], 0
        for chip_cap in range(40, 129, 2):
            for seed in range(3):
                try:
                    found.append(make_plan(ROUTE, CORES, writes, chip_cap, seed))
                except ValueError as err:
                    if "source" in str(err):
                        met = 3
                        break
            met += bool(found)
            if met >= 3:
                break
        if found:
            return min(found, key=lambda P: P["cost"])
    raise ValueError("no plan")


def send(g, core, T, topo, src, transfers):
    from concourse.bass import DstId, RemoteDMATransfer
    trs = []
    for j, (slot, dsts) in enumerate(transfers):
        ids = []
        for d, _ in dsts:
            rid, pid = topo.addr(d, core)
            ids.append(DstId(rid=rid, pnc=pid))
        trs.append(RemoteDMATransfer(dst_ids=ids, dma_engine_mask=1 << j, remote_sem=T.sem.arrived,
                                     srcs=[src[slot]], dsts=[T.land[x] for _, x in dsts]))
    g.remote_dma_fused(trs, local_sem=T.sem.sent)
    return len(trs)


def rank_program(g, core, T, topo):
    if "plan" not in CACHE:
        CACHE["plan"] = best_plan(T.tables["ROUTE"], list(T.cores))
    P = CACHE["plan"]
    rank = T.rank_of(core)
    due = P["arrive"].get(core, 0)
    if rank is None:
        if core in P["second"]:
            g.wait_ge(T.sem.arrived, due)
            g.wait_ge(T.sem.sent, send(g, core, T, topo, T.land, P["second"][core]))
        return
    g.dma_start(T.xs[:], T.x[:]).then_inc(T.sem.loaded, 16)
    loads = 16
    for t, rw, k in P["local"][core]:
        g.dma_start(T.land[rw:rw + k], T.x[t:t + k]).then_inc(T.sem.loaded, 16)
        loads += 16
    g.wait_ge(T.sem.loaded, loads)
    left = send(g, core, T, topo, T.xs, P["first"][core])
    g.wait_ge(T.sem.arrived, due)
    count = P["fill"][rank]
    g.dma_start(T.y[0:count], T.land[0:count]).then_inc(T.sem.stored, 16)
    g.wait_ge(T.sem.sent, left)
    g.wait_ge(T.sem.stored, 16)
